import numpy as np
import ml_dtypes


def mxq(x, axis, fmt="e4m3"):
    dtype, down = {"e4m3": (ml_dtypes.float8_e4m3fn, 7), "e5m2": (ml_dtypes.float8_e5m2, 14)}[fmt]
    v = np.moveaxis(np.asarray(x, np.float32).astype(ml_dtypes.bfloat16).astype(np.float64), axis, -1)
    blocks = v.reshape(v.shape[:-1] + (-1, 32))
    amax = np.abs(blocks).max(-1, keepdims=True)
    byte = np.maximum(np.where(amax > 0, np.frexp(amax)[1] - 1 + 127, 0) - down, 1)
    scale = np.exp2(byte - 127.0)
    codes = (blocks / scale).astype(np.float32).astype(dtype).astype(np.float64)
    return np.moveaxis((codes * scale).reshape(v.shape), -1, axis)


WIDE = False


def mx_kscale(k):
    if not WIDE:
        return np.ones(k)
    levels = np.array([10, -10, 5, -5, 0])
    if k % 512:
        return np.exp2(np.random.permutation(np.resize(levels, k // 32))).repeat(32)
    a = np.empty((k // 512, 16))
    for p in range(k // 512):
        a[p, :8] = np.random.permutation(np.resize(levels, 8))
        for g in range(8):
            far = levels[np.abs(levels - a[p, g]) >= 10]
            a[p, g + 8] = far[np.random.randint(len(far))]
    return np.exp2(a.ravel()).repeat(32)


def f64(x):
    return np.asarray(x).astype(np.float64)


def striped(idx):
    return np.tile(idx.reshape(-1, 16).T, (8, 1)).astype(np.uint16)


def unstriped(offs):
    return offs[:16].T.reshape(-1).astype(np.int64)


def striped8(idx):
    return np.concatenate([x.reshape(-1, 16).T for x in idx]).astype(np.uint16)


def runs(offs, k):
    lists = np.stack([offs[16 * r : 16 * r + 16].T.reshape(-1) for r in range(8)]).astype(np.int64)
    return lists[np.arange(k) % 512 // 64]


def pack_weight(w):
    k, n = w.shape
    w = f64(np.asarray(w, np.float32).astype(ml_dtypes.bfloat16)).reshape(k // 32, 32, n)
    amax = np.abs(w).max(1)
    byte = np.clip(np.where(amax > 0, np.frexp(amax)[1] - 1 + 127 - 7, 1), 1, 254)
    scaled = (w * np.exp2(127.0 - byte)[:, None, :]).reshape(k, n).astype(np.float32)
    words = np.ascontiguousarray(scaled.reshape(k // 512, 128, 4, n).transpose(0, 1, 3, 2)).astype(ml_dtypes.float8_e4m3fn).view(np.uint8)
    return words, np.ascontiguousarray(byte.astype(np.uint8).reshape(k // 512, 16, n))


def unpack_weight(words, scales):
    g, p, n, _ = words.shape
    vals = np.ascontiguousarray(words).view(ml_dtypes.float8_e4m3fn).astype(np.float64) * np.repeat(np.exp2(scales.astype(np.float64) - 127.0), 8, axis=1)[..., None]
    return vals.transpose(0, 1, 3, 2).reshape(g * 512, n)


E2M1 = np.array([0.0, 0.5, 1.0, 1.5, 2.0, 3.0, 4.0, 6.0, -0.0, -0.5, -1.0, -1.5, -2.0, -3.0, -4.0, -6.0])


def pack_fp4(w):
    k, n = w.shape
    w = f64(np.asarray(w, np.float32).astype(ml_dtypes.bfloat16)).reshape(k // 32, 32, n)
    amax = np.abs(w).max(1)
    mant, ex = np.frexp(amax / 6.0)
    byte = np.clip(np.where(amax > 0, np.where(mant > 0.5, ex, ex - 1) + 127, 1), 1, 254)
    scaled = (w * np.exp2(127.0 - byte)[:, None, :]).reshape(k, n).astype(np.float32)
    c = np.ascontiguousarray(scaled.reshape(k // 512, 128, 4, n).transpose(0, 1, 3, 2)).astype(ml_dtypes.float4_e2m1fn).view(np.uint8) & 0xF
    words = (c[..., 0::2] | (c[..., 1::2] << 4)).reshape(k // 512, 128, 2 * n)
    return np.ascontiguousarray(words), np.ascontiguousarray(byte.astype(np.uint8).reshape(k // 512, 16, n))


def unpack_fp4(words, scales):
    g, _, n = scales.shape
    words = np.ascontiguousarray(words).reshape(g, 128, n, 2)
    nib = np.empty((g, 128, n, 4), np.uint8)
    nib[..., 0::2] = words & 0xF
    nib[..., 1::2] = words >> 4
    vals = E2M1[nib] * np.repeat(np.exp2(scales.astype(np.float64) - 127.0), 8, axis=1)[..., None]
    return vals.transpose(0, 1, 3, 2).reshape(g * 512, n)


K, T, S, N, G, H, U = 512, 2048, 256, 512, 2048, 512, 512


def setup_inputs():
    n = np.random.standard_normal
    s = mx_kscale(K)[:, None]
    u = mx_kscale(K)
    packed_xT = pack_weight(n((K, T)) * s)
    packed_dT = pack_weight(n((K, G)) / s)
    packed_w1 = pack_fp4(n((H, N)) / np.sqrt(H) / u[:, None])
    perm = np.random.permutation(U)
    return {
        "x_words": packed_xT[0],
        "x_scales": packed_xT[1],
        "d_words": packed_dT[0],
        "d_scales": packed_dT[1],
        "gn": (np.random.uniform(0.5, 1.5, (H, 1)) * u[:, None]).astype(np.float32),
        "w1_words": packed_w1[0],
        "w1_scales": packed_w1[1],
        "offs": striped8(np.random.randint(0, T, (8, S))),
        "k1": striped8(np.random.randint(0, G, (8, H))),
        "n1": striped(perm[:S]),
        "n2": striped(perm[S:]),
        "n3": striped(np.random.permutation(S)),
    }


def reference(x_words, x_scales, d_words, d_scales, gn, w1_words, w1_scales, offs, k1, n1, n2, n3):
    d_k1 = unpack_weight(d_words, d_scales)[np.arange(K)[:, None], runs(k1, K)]
    xq = unpack_weight(x_words, x_scales)[np.arange(K)[:, None], runs(offs, K)]
    h = 0.0625 * (d_k1.T @ xq)
    z = f64(gn) * h
    h2 = unpack_fp4(w1_words, w1_scales).T @ mxq(z, 0, "e4m3")
    dn = np.minimum(h2, h2[:, unstriped(n3)])
    up = np.maximum(h2, h2[:, unstriped(n3)])
    ph = np.zeros((N, U))
    ph[:, unstriped(n1)] = up
    out = ph.copy()
    out[:, unstriped(n2)] = dn
    return out

@@ -1,0 +1,154 @@
+from contextlib import ExitStack
+
+import concourse.mybir as mybir
+
+K, T, S, N, G, H, U = 512, 2048, 256, 512, 2048, 512, 512
+FLOPS = 2 * K * H * S + 2 * H * N * S
+
+F32 = mybir.dt.float32
+BF16 = mybir.dt.bfloat16
+I32 = mybir.dt.int32
+U32 = mybir.dt.uint32
+U16 = mybir.dt.uint16
+U8 = mybir.dt.uint8
+FP8X4 = mybir.dt.float8_e4m3fn_x4
+FP4X4 = mybir.dt.float4_e2m1fn_x4
+ALU = mybir.AluOpType
+COPY = mybir.ActivationFunctionType.Copy
+
+P = 128
+PACK = 4
+HALF = S // 2
+SPARE = 8
+
+
+def tile_picked_hpqipagmx_none_p_kernel(
+    tc, x_words, x_scales, d_words, d_scales, gn, w1_words, w1_scales, offs, k1, n1, n2, n3, out
+):
+    nc = tc.nc
+    with ExitStack() as ctx:
+        keep = ctx.enter_context(tc.tile_pool(name="keep", bufs=1))
+        psum = ctx.enter_context(tc.psum_pool(name="psum", bufs=1))
+
+        k1_t = keep.tile([P, H // 16], U16, name="k1_t")
+        offs_t = keep.tile([P, S // 16], U16, name="offs_t")
+        n1_t = keep.tile([P, S // 16], U16, name="n1_t")
+        n2_t = keep.tile([P, S // 16], U16, name="n2_t")
+        n3_t = keep.tile([P, S // 16], U16, name="n3_t")
+        d_table = keep.tile([P, G], U32, name="d_table", align_bytes=64)
+        x_table = keep.tile([P, T], U32, name="x_table", align_bytes=64)
+        d_bytes = keep.tile([P, G], U8, name="d_bytes", align_bytes=64)
+        x_bytes = keep.tile([P, T], U8, name="x_bytes", align_bytes=64)
+        planes = keep.tile([P, H + S], U8, name="planes", align_bytes=64)
+        w1_plane = keep.tile([P, N], U8, name="w1_plane", align_bytes=64)
+        w1_codes = keep.tile([P, 2 * N], U8, name="w1_codes", align_bytes=64)
+        gain = keep.tile([P, PACK], F32, name="gain")
+        h2 = [keep.tile([P, S + SPARE], F32, name="h2_%d" % m) for m in range(N // P)]
+
+        nc.vector.memset(x_bytes[:].bitcast(I32), 0)
+        nc.gpsimd.memset(d_bytes[:].bitcast(I32), 0)
+        nc.vector.memset(w1_plane[:].bitcast(I32), 0)
+        nc.vector.memset(planes[:].bitcast(I32), 0)
+        for m in range(N // P):
+            nc.vector.memset(h2[m][:, S:], 0.0)
+
+        nc.sync.dma_start(offs_t[:], offs)
+        nc.sync.dma_start(k1_t[:], k1)
+        nc.sync.dma_start(d_bytes[0:P:8, :].bitcast(I32), d_scales[0].bitcast(I32))
+        nc.sync.dma_start(x_bytes[0:P:8, :].bitcast(I32), x_scales[0].bitcast(I32))
+        nc.sync.dma_start(n3_t[:], n3)
+        nc.sync.dma_start(n1_t[:], n1)
+        nc.sync.dma_start(n2_t[:], n2)
+        nc.sync.dma_start(d_table[:].bitcast(I32), d_words[0].rearrange("p n t -> p (n t)").bitcast(I32))
+        nc.sync.dma_start(x_table[:].bitcast(I32), x_words[0].rearrange("p n t -> p (n t)").bitcast(I32))
+        nc.gpsimd.dma_start(gain[:], gn.rearrange("(p t) o -> p (t o)", t=PACK))
+        nc.gpsimd.dma_start(w1_codes[:].bitcast(I32), w1_words[0].bitcast(I32))
+        for q in range(4):
+            nc.gpsimd.dma_start(
+                w1_plane[32 * q : 32 * q + 4, :].bitcast(I32), w1_scales[0, 4 * q : 4 * q + 4, :].bitcast(I32)
+            )
+
+        gain16 = keep.tile([P, PACK], F32, name="gain16")
+        nc.scalar.activation(gain16[:], gain[:], COPY, scale=0.0625)
+
+        x_picked_bytes = keep.tile([P, S], U8, name="x_picked_bytes", align_bytes=64)
+        d_picked_bytes = keep.tile([P, H], U8, name="d_picked_bytes", align_bytes=64)
+        staged = keep.tile([P, H + S], U8, name="staged", align_bytes=64)
+        nc.vector.tensor_copy(x_picked_bytes[:], x_bytes[:].indirect(offs_t[:]))
+        nc.vector.tensor_copy(d_picked_bytes[:], d_bytes[:].indirect(k1_t[:]))
+        nc.vector.tensor_copy(staged[:, H:].bitcast(I32), x_picked_bytes[:].bitcast(I32))
+        nc.vector.tensor_copy(
+            staged[:, :H].rearrange("p (t m) -> p t m", t=PACK),
+            d_picked_bytes[:].rearrange("p (m t) -> p t m", t=PACK),
+        )
+        for r in range(4):
+            queue = nc.scalar if r % 2 == 0 else nc.sync
+            queue.dma_start(planes[r:P:32, :].bitcast(I32), staged[8 * r : P : 32, :].bitcast(I32))
+
+        d_picked = keep.tile([P, H], U32, name="d_picked", align_bytes=64)
+        d_dealt = keep.tile([P, H], U32, name="d_dealt", align_bytes=64)
+        x_picked = keep.tile([P, S], U32, name="x_picked", align_bytes=64)
+        nc.vector.tensor_copy(d_picked[:], d_table[:].indirect(k1_t[:]))
+        nc.vector.tensor_copy(
+            d_dealt[:].rearrange("p (t m) -> p t m", t=PACK),
+            d_picked[:].rearrange("p (m t) -> p t m", t=PACK),
+        )
+        nc.vector.tensor_copy(x_picked[:], x_table[:].indirect(offs_t[:]))
+
+        z = [keep.tile([P, HALF, PACK], BF16, name="z_%d" % c, align_bytes=64) for c in range(2)]
+        z_codes = [keep.tile([P, HALF], U32, name="z_codes_%d" % c, align_bytes=64) for c in range(2)]
+        z_plane = [keep.tile([P, HALF], U8, name="z_plane_%d" % c, align_bytes=64) for c in range(2)]
+        h_bank = [psum.tile([P, PACK, HALF], F32, name="h_bank_%d" % c) for c in range(2)]
+        for c in range(2):
+            for t in range(PACK):
+                nc.tensor.matmul_mx(
+                    out=h_bank[c][:, t, :],
+                    lhsT=d_dealt[:, t * P : (t + 1) * P].bitcast(FP8X4),
+                    lhsT_scale=planes[:, t * P : (t + 1) * P],
+                    rhs=x_picked[:, c * HALF : (c + 1) * HALF].bitcast(FP8X4),
+                    rhs_scale=planes[:, H + c * HALF : H + (c + 1) * HALF],
+                    start=True,
+                    stop=True,
+                )
+        for c in range(2):
+            nc.vector.tensor_tensor(
+                z[c][:],
+                h_bank[c][:].rearrange("p t j -> p j t"),
+                gain16[:].unsqueeze(1).to_broadcast([P, HALF, PACK]),
+                ALU.mult,
+            )
+        for c in range(2):
+            nc.vector.quantize_mx(
+                out=z_codes[c][:].bitcast(FP8X4),
+                scales=z_plane[c][:],
+                in_=z[c][:].rearrange("p j t -> p (j t)"),
+            )
+
+        h2_bank = [psum.tile([P, S], F32, name="h2_bank_%d" % m) for m in range(N // P)]
+        for m in range(N // P):
+            for c in range(2):
+                nc.tensor.matmul_mx(
+                    out=h2_bank[m][:, c * HALF : (c + 1) * HALF],
+                    lhsT=w1_codes[:, 2 * P * m : 2 * P * (m + 1)].bitcast(FP4X4),
+                    lhsT_scale=w1_plane[:, P * m : P * (m + 1)],
+                    rhs=z_codes[c][:].bitcast(FP8X4),
+                    rhs_scale=z_plane[c][:],
+                    start=True,
+                    stop=True,
+                )
+
+        other = [keep.tile([P, S], F32, name="other_%d" % m) for m in range(N // P)]
+        up = [keep.tile([P, S], F32, name="up_%d" % m) for m in range(N // P)]
+        dn = [keep.tile([P, S], F32, name="dn_%d" % m) for m in range(N // P)]
+        page = [keep.tile([P, U], F32, name="page_%d" % m) for m in range(N // P)]
+        for m in range(N // P):
+            nc.vector.tensor_copy(h2[m][:, :S], h2_bank[m][:])
+            nc.scalar.activation(other[m][:], h2[m][:].indirect(n3_t[:]), COPY)
+            nc.vector.tensor_tensor(up[m][:], h2[m][:, :S], other[m][:], ALU.max)
+            nc.vector.tensor_tensor(dn[m][:], h2[m][:, :S], other[m][:], ALU.min)
+        for pair in range(0, N // P, 2):
+            for m in (pair, pair + 1):
+                nc.scalar.activation(page[m][:].indirect(n1_t[:]), up[m][:], COPY)
+            for m in (pair, pair + 1):
+                nc.scalar.activation(page[m][:].indirect(n2_t[:]), dn[m][:], COPY)
+                nc.sync.dma_start(out[P * m : P * (m + 1), :], page[m][:])

@@ -20,6 +20,7 @@ P = 128
 PACK = 4
 HALF = S // 2
 SPARE = 8
+LEAD = 512
 
 
 def tile_picked_hpqipagmx_none_p_kernel(
@@ -40,58 +41,58 @@ def tile_picked_hpqipagmx_none_p_kernel(
         d_bytes = keep.tile([P, G], U8, name="d_bytes", align_bytes=64)
         x_bytes = keep.tile([P, T], U8, name="x_bytes", align_bytes=64)
         planes = keep.tile([P, H + S], U8, name="planes", align_bytes=64)
-        w1_plane = keep.tile([P, N], U8, name="w1_plane", align_bytes=64)
         w1_codes = keep.tile([P, 2 * N], U8, name="w1_codes", align_bytes=64)
         gain = keep.tile([P, PACK], F32, name="gain")
         h2 = [keep.tile([P, S + SPARE], F32, name="h2_%d" % m) for m in range(N // P)]
 
-        nc.vector.memset(x_bytes[:].bitcast(I32), 0)
-        nc.gpsimd.memset(d_bytes[:].bitcast(I32), 0)
-        nc.vector.memset(w1_plane[:].bitcast(I32), 0)
-        nc.vector.memset(planes[:].bitcast(I32), 0)
+        nc.vector.memset(d_bytes[:].bitcast(I32), 0)
+        nc.gpsimd.memset(x_bytes[:].bitcast(I32), 0)
         for m in range(N // P):
             nc.vector.memset(h2[m][:, S:], 0.0)
 
-        nc.sync.dma_start(offs_t[:], offs)
+        d_rows = d_words[0].rearrange("p n t -> p (n t)").bitcast(I32)
         nc.sync.dma_start(k1_t[:], k1)
+        nc.sync.dma_start(offs_t[:], offs)
         nc.sync.dma_start(d_bytes[0:P:8, :].bitcast(I32), d_scales[0].bitcast(I32))
         nc.sync.dma_start(x_bytes[0:P:8, :].bitcast(I32), x_scales[0].bitcast(I32))
+        nc.sync.dma_start(d_table[:, :LEAD].bitcast(I32), d_rows[:, :LEAD])
+        nc.sync.dma_start(gain[:], gn.rearrange("(p t) o -> p (t o)", t=PACK))
         nc.sync.dma_start(n3_t[:], n3)
+        nc.sync.dma_start(d_table[:, LEAD:].bitcast(I32), d_rows[:, LEAD:])
+        nc.sync.dma_start(x_table[:].bitcast(I32), x_words[0].rearrange("p n t -> p (n t)").bitcast(I32))
         nc.sync.dma_start(n1_t[:], n1)
         nc.sync.dma_start(n2_t[:], n2)
-        nc.sync.dma_start(d_table[:].bitcast(I32), d_words[0].rearrange("p n t -> p (n t)").bitcast(I32))
-        nc.sync.dma_start(x_table[:].bitcast(I32), x_words[0].rearrange("p n t -> p (n t)").bitcast(I32))
-        nc.gpsimd.dma_start(gain[:], gn.rearrange("(p t) o -> p (t o)", t=PACK))
-        nc.gpsimd.dma_start(w1_codes[:].bitcast(I32), w1_words[0].bitcast(I32))
-        for q in range(4):
-            nc.gpsimd.dma_start(
-                w1_plane[32 * q : 32 * q + 4, :].bitcast(I32), w1_scales[0, 4 * q : 4 * q + 4, :].bitcast(I32)
-            )
+        nc.sync.dma_start(w1_codes[:].bitcast(I32), w1_words[0].bitcast(I32))
 
         gain16 = keep.tile([P, PACK], F32, name="gain16")
         nc.scalar.activation(gain16[:], gain[:], COPY, scale=0.0625)
 
         x_picked_bytes = keep.tile([P, S], U8, name="x_picked_bytes", align_bytes=64)
         d_picked_bytes = keep.tile([P, H], U8, name="d_picked_bytes", align_bytes=64)
-        staged = keep.tile([P, H + S], U8, name="staged", align_bytes=64)
-        nc.vector.tensor_copy(x_picked_bytes[:], x_bytes[:].indirect(offs_t[:]))
+        staged = keep.tile([P, H + S], U8, name="staged", tag="scale_rows", align_bytes=64)
         nc.vector.tensor_copy(d_picked_bytes[:], d_bytes[:].indirect(k1_t[:]))
-        nc.vector.tensor_copy(staged[:, H:].bitcast(I32), x_picked_bytes[:].bitcast(I32))
+        nc.vector.tensor_copy(x_picked_bytes[:], x_bytes[:].indirect(offs_t[:]))
         nc.vector.tensor_copy(
             staged[:, :H].rearrange("p (t m) -> p t m", t=PACK),
             d_picked_bytes[:].rearrange("p (m t) -> p t m", t=PACK),
         )
+        nc.vector.tensor_copy(staged[:, H:].bitcast(I32), x_picked_bytes[:].bitcast(I32))
         for r in range(4):
-            queue = nc.scalar if r % 2 == 0 else nc.sync
-            queue.dma_start(planes[r:P:32, :].bitcast(I32), staged[8 * r : P : 32, :].bitcast(I32))
+            nc.scalar.dma_start(planes[r:P:32, :].bitcast(I32), staged[8 * r : P : 32, :].bitcast(I32))
+        w1_plane = keep.tile([P, N], U8, name="w1_plane", tag="scale_rows", align_bytes=64)
+        for q in range(4):
+            queue = nc.sync if q % 2 == 0 else nc.scalar
+            queue.dma_start(
+                w1_plane[32 * q : 32 * q + 4, :].bitcast(I32), w1_scales[0, 4 * q : 4 * q + 4, :].bitcast(I32)
+            )
 
         d_picked = keep.tile([P, H], U32, name="d_picked", align_bytes=64)
         d_dealt = keep.tile([P, H], U32, name="d_dealt", align_bytes=64)
         x_picked = keep.tile([P, S], U32, name="x_picked", align_bytes=64)
         nc.vector.tensor_copy(d_picked[:], d_table[:].indirect(k1_t[:]))
         nc.vector.tensor_copy(
-            d_dealt[:].rearrange("p (t m) -> p t m", t=PACK),
-            d_picked[:].rearrange("p (m t) -> p t m", t=PACK),
+            d_dealt[:].rearrange("p (t m) -> p m t", t=PACK),
+            d_picked[:].rearrange("p (m t) -> p m t", t=PACK),
         )
         nc.vector.tensor_copy(x_picked[:], x_table[:].indirect(offs_t[:]))
 
@@ -124,11 +125,13 @@ def tile_picked_hpqipagmx_none_p_kernel(
                 in_=z[c][:].rearrange("p j t -> p (j t)"),
             )
 
-        h2_bank = [psum.tile([P, S], F32, name="h2_bank_%d" % m) for m in range(N // P)]
+        first_bank = [psum.tile([P, HALF], F32, name="first_bank_%d" % c) for c in range(2)]
+        later_bank = [psum.tile([P, S], F32, name="later_bank_%d" % m) for m in range(1, N // P)]
         for m in range(N // P):
             for c in range(2):
+                sums = first_bank[c][:] if m == 0 else later_bank[m - 1][:, c * HALF : (c + 1) * HALF]
                 nc.tensor.matmul_mx(
-                    out=h2_bank[m][:, c * HALF : (c + 1) * HALF],
+                    out=sums,
                     lhsT=w1_codes[:, 2 * P * m : 2 * P * (m + 1)].bitcast(FP4X4),
                     lhsT_scale=w1_plane[:, P * m : P * (m + 1)],
                     rhs=z_codes[c][:].bitcast(FP8X4),
@@ -141,12 +144,17 @@ def tile_picked_hpqipagmx_none_p_kernel(
         up = [keep.tile([P, S], F32, name="up_%d" % m) for m in range(N // P)]
         dn = [keep.tile([P, S], F32, name="dn_%d" % m) for m in range(N // P)]
         page = [keep.tile([P, U], F32, name="page_%d" % m) for m in range(N // P)]
+        nc.scalar.copy(h2[0][:, :HALF], first_bank[0][:])
+        nc.vector.tensor_copy(h2[0][:, HALF:S], first_bank[1][:])
+        for m in range(1, N // P):
+            nc.vector.tensor_copy(h2[m][:, :S], later_bank[m - 1][:])
         for m in range(N // P):
-            nc.vector.tensor_copy(h2[m][:, :S], h2_bank[m][:])
             nc.scalar.activation(other[m][:], h2[m][:].indirect(n3_t[:]), COPY)
-            nc.vector.tensor_tensor(up[m][:], h2[m][:, :S], other[m][:], ALU.max)
-            nc.vector.tensor_tensor(dn[m][:], h2[m][:, :S], other[m][:], ALU.min)
         for pair in range(0, N // P, 2):
+            for m in (pair, pair + 1):
+                nc.vector.tensor_tensor(up[m][:], h2[m][:, :S], other[m][:], ALU.max)
+            for m in (pair, pair + 1):
+                nc.vector.tensor_tensor(dn[m][:], h2[m][:, :S], other[m][:], ALU.min)
             for m in (pair, pair + 1):
                 nc.scalar.activation(page[m][:].indirect(n1_t[:]), up[m][:], COPY)
             for m in (pair, pair + 1):

@@ -20,7 +20,7 @@ P = 128
 PACK = 4
 HALF = S // 2
 SPARE = 8
-LEAD = 512
+LEAD = 256
 
 
 def tile_picked_hpqipagmx_none_p_kernel(
@@ -41,7 +41,6 @@ def tile_picked_hpqipagmx_none_p_kernel(
         d_bytes = keep.tile([P, G], U8, name="d_bytes", align_bytes=64)
         x_bytes = keep.tile([P, T], U8, name="x_bytes", align_bytes=64)
         planes = keep.tile([P, H + S], U8, name="planes", align_bytes=64)
-        w1_codes = keep.tile([P, 2 * N], U8, name="w1_codes", align_bytes=64)
         gain = keep.tile([P, PACK], F32, name="gain")
         h2 = [keep.tile([P, S + SPARE], F32, name="h2_%d" % m) for m in range(N // P)]
 
@@ -51,23 +50,22 @@ def tile_picked_hpqipagmx_none_p_kernel(
             nc.vector.memset(h2[m][:, S:], 0.0)
 
         d_rows = d_words[0].rearrange("p n t -> p (n t)").bitcast(I32)
+        nc.scalar.dma_start(gain[:], gn.rearrange("(p t) o -> p (t o)", t=PACK))
         nc.sync.dma_start(k1_t[:], k1)
         nc.sync.dma_start(offs_t[:], offs)
         nc.sync.dma_start(d_bytes[0:P:8, :].bitcast(I32), d_scales[0].bitcast(I32))
         nc.sync.dma_start(x_bytes[0:P:8, :].bitcast(I32), x_scales[0].bitcast(I32))
         nc.sync.dma_start(d_table[:, :LEAD].bitcast(I32), d_rows[:, :LEAD])
-        nc.sync.dma_start(gain[:], gn.rearrange("(p t) o -> p (t o)", t=PACK))
         nc.sync.dma_start(n3_t[:], n3)
         nc.sync.dma_start(d_table[:, LEAD:].bitcast(I32), d_rows[:, LEAD:])
         nc.sync.dma_start(x_table[:].bitcast(I32), x_words[0].rearrange("p n t -> p (n t)").bitcast(I32))
         nc.sync.dma_start(n1_t[:], n1)
         nc.sync.dma_start(n2_t[:], n2)
-        nc.sync.dma_start(w1_codes[:].bitcast(I32), w1_words[0].bitcast(I32))
 
         gain16 = keep.tile([P, PACK], F32, name="gain16")
         nc.scalar.activation(gain16[:], gain[:], COPY, scale=0.0625)
 
-        x_picked_bytes = keep.tile([P, S], U8, name="x_picked_bytes", align_bytes=64)
+        x_picked_bytes = keep.tile([P, S], U8, name="x_picked_bytes", tag="w1_bytes", align_bytes=64)
         d_picked_bytes = keep.tile([P, H], U8, name="d_picked_bytes", align_bytes=64)
         staged = keep.tile([P, H + S], U8, name="staged", tag="scale_rows", align_bytes=64)
         nc.vector.tensor_copy(d_picked_bytes[:], d_bytes[:].indirect(k1_t[:]))
@@ -78,7 +76,10 @@ def tile_picked_hpqipagmx_none_p_kernel(
         )
         nc.vector.tensor_copy(staged[:, H:].bitcast(I32), x_picked_bytes[:].bitcast(I32))
         for r in range(4):
-            nc.scalar.dma_start(planes[r:P:32, :].bitcast(I32), staged[8 * r : P : 32, :].bitcast(I32))
+            queue = nc.scalar if r % 2 == 0 else nc.sync
+            queue.dma_start(planes[r:P:32, :].bitcast(I32), staged[8 * r : P : 32, :].bitcast(I32))
+        w1_codes = keep.tile([P, 2 * N], U8, name="w1_codes", tag="w1_bytes", align_bytes=64)
+        nc.sync.dma_start(w1_codes[:].bitcast(I32), w1_words[0].bitcast(I32))
         w1_plane = keep.tile([P, N], U8, name="w1_plane", tag="scale_rows", align_bytes=64)
         for q in range(4):
             queue = nc.sync if q % 2 == 0 else nc.scalar
@@ -159,4 +160,5 @@ def tile_picked_hpqipagmx_none_p_kernel(
                 nc.scalar.activation(page[m][:].indirect(n1_t[:]), up[m][:], COPY)
             for m in (pair, pair + 1):
                 nc.scalar.activation(page[m][:].indirect(n2_t[:]), dn[m][:], COPY)
-                nc.sync.dma_start(out[P * m : P * (m + 1), :], page[m][:])
+                queue = nc.scalar if m == N // P - 1 else nc.sync
+                queue.dma_start(out[P * m : P * (m + 1), :], page[m][:])

from contextlib import ExitStack

import concourse.mybir as mybir

K, T, S, N, G, H, U = 512, 2048, 256, 512, 2048, 512, 512
FLOPS = 2 * K * H * S + 2 * H * N * S

F32 = mybir.dt.float32
BF16 = mybir.dt.bfloat16
I32 = mybir.dt.int32
U32 = mybir.dt.uint32
U16 = mybir.dt.uint16
U8 = mybir.dt.uint8
FP8X4 = mybir.dt.float8_e4m3fn_x4
FP4X4 = mybir.dt.float4_e2m1fn_x4
ALU = mybir.AluOpType
COPY = mybir.ActivationFunctionType.Copy

P = 128
PACK = 4
HALF = S // 2
SPARE = 8
LEAD = 256


def tile_picked_hpqipagmx_none_p_kernel(
    tc, x_words, x_scales, d_words, d_scales, gn, w1_words, w1_scales, offs, k1, n1, n2, n3, out
):
    nc = tc.nc
    with ExitStack() as ctx:
        keep = ctx.enter_context(tc.tile_pool(name="keep", bufs=1))
        psum = ctx.enter_context(tc.psum_pool(name="psum", bufs=1))

        k1_t = keep.tile([P, H // 16], U16, name="k1_t")
        offs_t = keep.tile([P, S // 16], U16, name="offs_t")
        n1_t = keep.tile([P, S // 16], U16, name="n1_t")
        n2_t = keep.tile([P, S // 16], U16, name="n2_t")
        n3_t = keep.tile([P, S // 16], U16, name="n3_t")
        d_table = keep.tile([P, G], U32, name="d_table", align_bytes=64)
        x_table = keep.tile([P, T], U32, name="x_table", align_bytes=64)
        d_bytes = keep.tile([P, G], U8, name="d_bytes", align_bytes=64)
        x_bytes = keep.tile([P, T], U8, name="x_bytes", align_bytes=64)
        planes = keep.tile([P, H + S], U8, name="planes", align_bytes=64)
        gain = keep.tile([P, PACK], F32, name="gain")
        h2 = [keep.tile([P, S + SPARE], F32, name="h2_%d" % m) for m in range(N // P)]

        nc.vector.memset(d_bytes[:].bitcast(I32), 0)
        nc.gpsimd.memset(x_bytes[:].bitcast(I32), 0)
        for m in range(N // P):
            nc.vector.memset(h2[m][:, S:], 0.0)

        d_rows = d_words[0].rearrange("p n t -> p (n t)").bitcast(I32)
        nc.scalar.dma_start(gain[:], gn.rearrange("(p t) o -> p (t o)", t=PACK))
        nc.sync.dma_start(k1_t[:], k1)
        nc.sync.dma_start(offs_t[:], offs)
        nc.sync.dma_start(d_bytes[0:P:8, :].bitcast(I32), d_scales[0].bitcast(I32))
        nc.sync.dma_start(x_bytes[0:P:8, :].bitcast(I32), x_scales[0].bitcast(I32))
        nc.sync.dma_start(d_table[:, :LEAD].bitcast(I32), d_rows[:, :LEAD])
        nc.sync.dma_start(n3_t[:], n3)
        nc.sync.dma_start(d_table[:, LEAD:].bitcast(I32), d_rows[:, LEAD:])
        nc.sync.dma_start(x_table[:].bitcast(I32), x_words[0].rearrange("p n t -> p (n t)").bitcast(I32))
        nc.sync.dma_start(n1_t[:], n1)
        nc.sync.dma_start(n2_t[:], n2)

        gain16 = keep.tile([P, PACK], F32, name="gain16")
        nc.scalar.activation(gain16[:], gain[:], COPY, scale=0.0625)

        x_picked_bytes = keep.tile([P, S], U8, name="x_picked_bytes", tag="w1_bytes", align_bytes=64)
        d_picked_bytes = keep.tile([P, H], U8, name="d_picked_bytes", align_bytes=64)
        staged = keep.tile([P, H + S], U8, name="staged", tag="scale_rows", align_bytes=64)
        nc.vector.tensor_copy(d_picked_bytes[:], d_bytes[:].indirect(k1_t[:]))
        nc.vector.tensor_copy(x_picked_bytes[:], x_bytes[:].indirect(offs_t[:]))
        nc.vector.tensor_copy(
            staged[:, :H].rearrange("p (t m) -> p t m", t=PACK),
            d_picked_bytes[:].rearrange("p (m t) -> p t m", t=PACK),
        )
        nc.vector.tensor_copy(staged[:, H:].bitcast(I32), x_picked_bytes[:].bitcast(I32))
        for r in range(4):
            queue = nc.scalar if r % 2 == 0 else nc.sync
            queue.dma_start(planes[r:P:32, :].bitcast(I32), staged[8 * r : P : 32, :].bitcast(I32))
        w1_codes = keep.tile([P, 2 * N], U8, name="w1_codes", tag="w1_bytes", align_bytes=64)
        nc.sync.dma_start(w1_codes[:].bitcast(I32), w1_words[0].bitcast(I32))
        w1_plane = keep.tile([P, N], U8, name="w1_plane", tag="scale_rows", align_bytes=64)
        for q in range(4):
            queue = nc.sync if q % 2 == 0 else nc.scalar
            queue.dma_start(
                w1_plane[32 * q : 32 * q + 4, :].bitcast(I32), w1_scales[0, 4 * q : 4 * q + 4, :].bitcast(I32)
            )

        d_picked = keep.tile([P, H], U32, name="d_picked", align_bytes=64)
        d_dealt = keep.tile([P, H], U32, name="d_dealt", align_bytes=64)
        x_picked = keep.tile([P, S], U32, name="x_picked", align_bytes=64)
        nc.vector.tensor_copy(d_picked[:], d_table[:].indirect(k1_t[:]))
        nc.vector.tensor_copy(
            d_dealt[:].rearrange("p (t m) -> p m t", t=PACK),
            d_picked[:].rearrange("p (m t) -> p m t", t=PACK),
        )
        nc.vector.tensor_copy(x_picked[:], x_table[:].indirect(offs_t[:]))

        z = [keep.tile([P, HALF, PACK], BF16, name="z_%d" % c, align_bytes=64) for c in range(2)]
        z_codes = [keep.tile([P, HALF], U32, name="z_codes_%d" % c, align_bytes=64) for c in range(2)]
        z_plane = [keep.tile([P, HALF], U8, name="z_plane_%d" % c, align_bytes=64) for c in range(2)]
        h_bank = [psum.tile([P, PACK, HALF], F32, name="h_bank_%d" % c) for c in range(2)]
        for c in range(2):
            for t in range(PACK):
                nc.tensor.matmul_mx(
                    out=h_bank[c][:, t, :],
                    lhsT=d_dealt[:, t * P : (t + 1) * P].bitcast(FP8X4),
                    lhsT_scale=planes[:, t * P : (t + 1) * P],
                    rhs=x_picked[:, c * HALF : (c + 1) * HALF].bitcast(FP8X4),
                    rhs_scale=planes[:, H + c * HALF : H + (c + 1) * HALF],
                    start=True,
                    stop=True,
                )
        for c in range(2):
            nc.vector.tensor_tensor(
                z[c][:],
                h_bank[c][:].rearrange("p t j -> p j t"),
                gain16[:].unsqueeze(1).to_broadcast([P, HALF, PACK]),
                ALU.mult,
            )
        for c in range(2):
            nc.vector.quantize_mx(
                out=z_codes[c][:].bitcast(FP8X4),
                scales=z_plane[c][:],
                in_=z[c][:].rearrange("p j t -> p (j t)"),
            )

        first_bank = [psum.tile([P, HALF], F32, name="first_bank_%d" % c) for c in range(2)]
        later_bank = [psum.tile([P, S], F32, name="later_bank_%d" % m) for m in range(1, N // P)]
        for m in range(N // P):
            for c in range(2):
                sums = first_bank[c][:] if m == 0 else later_bank[m - 1][:, c * HALF : (c + 1) * HALF]
                nc.tensor.matmul_mx(
                    out=sums,
                    lhsT=w1_codes[:, 2 * P * m : 2 * P * (m + 1)].bitcast(FP4X4),
                    lhsT_scale=w1_plane[:, P * m : P * (m + 1)],
                    rhs=z_codes[c][:].bitcast(FP8X4),
                    rhs_scale=z_plane[c][:],
                    start=True,
                    stop=True,
                )

        other = [keep.tile([P, S], F32, name="other_%d" % m) for m in range(N // P)]
        up = [keep.tile([P, S], F32, name="up_%d" % m) for m in range(N // P)]
        dn = [keep.tile([P, S], F32, name="dn_%d" % m) for m in range(N // P)]
        page = [keep.tile([P, U], F32, name="page_%d" % m) for m in range(N // P)]
        nc.scalar.copy(h2[0][:, :HALF], first_bank[0][:])
        nc.vector.tensor_copy(h2[0][:, HALF:S], first_bank[1][:])
        for m in range(1, N // P):
            nc.vector.tensor_copy(h2[m][:, :S], later_bank[m - 1][:])
        for m in range(N // P):
            nc.scalar.activation(other[m][:], h2[m][:].indirect(n3_t[:]), COPY)
        for pair in range(0, N // P, 2):
            for m in (pair, pair + 1):
                nc.vector.tensor_tensor(up[m][:], h2[m][:, :S], other[m][:], ALU.max)
            for m in (pair, pair + 1):
                nc.vector.tensor_tensor(dn[m][:], h2[m][:, :S], other[m][:], ALU.min)
            for m in (pair, pair + 1):
                nc.scalar.activation(page[m][:].indirect(n1_t[:]), up[m][:], COPY)
            for m in (pair, pair + 1):
                nc.scalar.activation(page[m][:].indirect(n2_t[:]), dn[m][:], COPY)
                queue = nc.scalar if m == N // P - 1 else nc.sync
                queue.dma_start(out[P * m : P * (m + 1), :], page[m][:])
